import numpy as np
import ml_dtypes


def mxq(x, axis, fmt="e4m3"):
    dtype, down = {"e4m3": (ml_dtypes.float8_e4m3fn, 7), "e5m2": (ml_dtypes.float8_e5m2, 14)}[fmt]
    v = np.moveaxis(np.asarray(x, np.float32).astype(ml_dtypes.bfloat16).astype(np.float64), axis, -1)
    blocks = v.reshape(v.shape[:-1] + (-1, 32))
    amax = np.abs(blocks).max(-1, keepdims=True)
    byte = np.maximum(np.where(amax > 0, np.frexp(amax)[1] - 1 + 127, 0) - down, 1)
    scale = np.exp2(byte - 127.0)
    codes = (blocks / scale).astype(np.float32).astype(dtype).astype(np.float64)
    return np.moveaxis((codes * scale).reshape(v.shape), -1, axis)


WIDE = False


def mx_kscale(k):
    if not WIDE:
        return np.ones(k)
    levels = np.array([10, -10, 5, -5, 0])
    if k % 512:
        return np.exp2(np.random.permutation(np.resize(levels, k // 32))).repeat(32)
    a = np.empty((k // 512, 16))
    for p in range(k // 512):
        a[p, :8] = np.random.permutation(np.resize(levels, 8))
        for g in range(8):
            far = levels[np.abs(levels - a[p, g]) >= 10]
            a[p, g + 8] = far[np.random.randint(len(far))]
    return np.exp2(a.ravel()).repeat(32)


def f64(x):
    return np.asarray(x).astype(np.float64)


def striped(idx):
    return np.tile(np.asarray(idx).reshape(-1, 16).T, (8, 1)).astype(np.uint16)


def unstriped(offs):
    return offs[:16].T.reshape(-1).astype(np.int64)


E2M1 = np.array([0.0, 0.5, 1.0, 1.5, 2.0, 3.0, 4.0, 6.0, -0.0, -0.5, -1.0, -1.5, -2.0, -3.0, -4.0, -6.0])


def pack_weight(w, fmt):
    k, n = w.shape
    w = f64(np.asarray(w, np.float32).astype(ml_dtypes.bfloat16)).reshape(k // 32, 32, n)
    amax = np.abs(w).max(1)
    if fmt == "e4m3":
        byte = np.frexp(amax)[1] - 1 + 127 - 7
    else:
        mant, ex = np.frexp(amax / 6.0)
        byte = np.where(mant > 0.5, ex, ex - 1) + 127
    byte = np.clip(np.where(amax > 0, byte, 1), 1, 254)
    scaled = (w * np.exp2(127.0 - byte)[:, None, :]).reshape(k, n).astype(np.float32)
    by_word = np.ascontiguousarray(scaled.reshape(k // 512, 128, 4, n).transpose(0, 1, 3, 2))
    if fmt == "e4m3":
        words = by_word.astype(ml_dtypes.float8_e4m3fn).view(np.uint8)
    else:
        c = by_word.astype(ml_dtypes.float4_e2m1fn).view(np.uint8) & 0xF
        words = (c[..., 0::2] | (c[..., 1::2] << 4)).reshape(k // 512, 128, 2 * n)
    return np.ascontiguousarray(words), np.ascontiguousarray(byte.astype(np.uint8).reshape(k // 512, 16, n))


def unpack_weight(words, scales, fmt):
    g, _, n = scales.shape
    words = np.ascontiguousarray(words).reshape(g, 128, n, -1)
    if fmt == "e4m3":
        vals = words.view(ml_dtypes.float8_e4m3fn).astype(np.float64)
    else:
        nib = np.empty((g, 128, n, 4), np.uint8)
        nib[..., 0::2] = words & 0xF
        nib[..., 1::2] = words >> 4
        vals = E2M1[nib]
    vals = vals * np.repeat(np.exp2(scales.astype(np.float64) - 127.0), 8, axis=1)[..., None]
    return vals.transpose(0, 1, 3, 2).reshape(g * 512, n)


def sigmoid(v):
    return 1.0 / (1.0 + np.exp(-v))


K, U, I, T, E = 512, 2048, 512, 1024, 512


def setup_inputs():
    n = np.random.standard_normal
    idx = np.random.permutation(T)[:I]
    idx2 = np.random.permutation(U)[:I]
    fk = mx_kscale(K)
    hidp = pack_weight(n((K, U)) / fk[:, None], "e2m1")
    return {
        "wv": (n((K, E)) * 1 / np.sqrt(K) * fk[:, None]).astype(np.float32),
        "hid_words": hidp[0],
        "hid_scales": hidp[1],
        "store": (n((E, T))).astype(np.float32),
        "rate": (np.random.uniform(0.3, 1.0, (1, I))).astype(np.float32),
        "offs": striped(idx),
        "offs2": striped(idx2),
    }


def reference(wv, hid_words, hid_scales, store, rate, offs, offs2):
    idx = unstriped(offs)
    idx2 = unstriped(offs2)
    hidu = unpack_weight(hid_words, hid_scales, "e2m1")
    wvq = mxq(f64(wv), 0, "e4m3")
    hididx2g = hidu[:, idx2]
    v = wvq.T @ hididx2g
    dl = (v - f64(store)[:, idx]) * f64(rate) * sigmoid(f64(store)[:, idx])
    df = np.zeros((E, T))
    df[:, idx] = dl
    y = f64(store) + df
    return y

@@ -1,0 +1,153 @@
+from contextlib import ExitStack
+
+import concourse.mybir as mybir
+from concourse.masks import make_identity
+
+K, U, SLOTS, T, E = 512, 2048, 512, 1024, 512
+FLOPS = 2 * K * E * SLOTS
+
+F32 = mybir.dt.float32
+BF16 = mybir.dt.bfloat16
+I32 = mybir.dt.int32
+U32 = mybir.dt.uint32
+U16 = mybir.dt.uint16
+U8 = mybir.dt.uint8
+FP8X4 = mybir.dt.float8_e4m3fn_x4
+FP4X4 = mybir.dt.float4_e2m1fn_x4
+ALU = mybir.AluOpType
+ACT = mybir.ActivationFunctionType
+
+P = 128
+PACK = 4
+BANK = 512
+TILES = E // P
+HALF = E // 2
+
+
+def tile_attend_storeblend_kernel(tc, wv, hid_words, hid_scales, store, rate, offs, offs2, out):
+    nc = tc.nc
+    with ExitStack() as ctx:
+        keep = ctx.enter_context(tc.tile_pool(name="keep", bufs=1))
+        work = ctx.enter_context(tc.tile_pool(name="work", bufs=4))
+        psum = ctx.enter_context(tc.psum_pool(name="psum", bufs=2))
+
+        place_list = keep.tile([P, SLOTS // 16], U16, name="place_list")
+        token_list = keep.tile([P, SLOTS // 16], U16, name="token_list")
+        words = keep.tile([P, U], U16, name="words", align_bytes=64)
+        scale_rows = keep.tile([P, U], U8, name="scale_rows", align_bytes=64)
+        held = [keep.tile([P, T], F32, name=f"held{n}") for n in range(TILES)]
+        moved = [keep.tile([P, T], F32, name=f"moved{n}") for n in range(TILES)]
+        wv_raw = [keep.tile([P, PACK, HALF], F32, name=f"wv_raw{h}") for h in range(2)]
+        rate_cols = keep.tile([P, PACK], F32, name="rate_cols")
+        ident = keep.tile([P, P], F32, name="ident")
+        warm = keep.tile([P, 1], F32, name="warm")
+
+        nc.gpsimd.memset(scale_rows[:].bitcast(I32), 0)
+        make_identity(nc, ident[:])
+        for n in range(TILES):
+            engine = nc.vector if n < 2 else nc.gpsimd
+            engine.memset(moved[n][:], 0.0)
+
+        wv_rows = wv.rearrange("(p j) e -> p j e", j=PACK)
+        for q in range(4):
+            nc.scalar.dma_start(
+                scale_rows[32 * q : 32 * q + 4, :].bitcast(I32), hid_scales[0, 4 * q : 4 * q + 4, :].bitcast(I32)
+            )
+        nc.sync.dma_start(rate_cols[:], rate.rearrange("o (p j) -> (o p) j", j=PACK))
+        nc.scalar.activation(warm[:], rate_cols[:, 0:1], ACT.Sigmoid)
+        nc.sync.dma_start(held[0][:], store[0:P, :])
+        nc.sync.dma_start(place_list[:], offs)
+        nc.sync.dma_start(token_list[:], offs2)
+        nc.sync.dma_start(words[:].bitcast(I32), hid_words[0].bitcast(I32))
+        for h in range(2):
+            nc.sync.dma_start(wv_raw[h][:], wv_rows[:, :, h * HALF : (h + 1) * HALF])
+        for n in range(1, TILES):
+            nc.sync.dma_start(held[n][:], store[n * P : (n + 1) * P, :])
+
+        first_old = keep.tile([P, SLOTS], F32, name="first_old")
+        nc.vector.tensor_copy(first_old[:], held[0][:].indirect(place_list[:]))
+
+        hid_codes = keep.tile([P, SLOTS], U16, name="hid_codes", align_bytes=64)
+        hid_plane = keep.tile([P, SLOTS], U8, name="hid_plane", align_bytes=64)
+        nc.vector.tensor_copy(hid_plane[:], scale_rows[:].indirect(token_list[:]))
+        nc.vector.tensor_copy(hid_codes[:], words[:].indirect(token_list[:]))
+
+        rate_bank = psum.tile([P, PACK, P], F32, name="rate_bank", tag="back")
+        for j in range(PACK):
+            nc.tensor.transpose(rate_bank[:, j, :], rate_cols[:, j : j + 1].to_broadcast([P, P]), ident[:])
+        rate_rows = keep.tile([P, P, PACK], F32, name="rate_rows")
+        nc.scalar.activation(rate_rows[:], rate_bank[:].rearrange("p j n -> p n j"), ACT.Copy, scale=-1.0)
+
+        def project(n):
+            h, c0 = divmod(n * P, HALF)
+            grouped = work.tile([P, P, PACK], BF16, name="grouped", align_bytes=64)
+            nc.scalar.copy(
+                grouped[:].rearrange("p (c i) j -> p c j i", i=4),
+                wv_raw[h][:, :, c0 : c0 + P].rearrange("p j (c i) -> p c j i", i=4),
+            )
+            wv_codes = work.tile([P, P], U32, name="wv_codes", align_bytes=64)
+            wv_plane = work.tile([P, P], U8, name="wv_plane", align_bytes=64)
+            nc.vector.quantize_mx(
+                out=wv_codes[:].bitcast(FP8X4), scales=wv_plane[:], in_=grouped[:].rearrange("p c j -> p (c j)")
+            )
+            sums = psum.tile([P, SLOTS], F32, name="sums", tag=f"bank{n}", bufs=1)
+            nc.tensor.matmul_mx(
+                out=sums[:],
+                lhsT=wv_codes[:].bitcast(FP8X4),
+                lhsT_scale=wv_plane[:],
+                rhs=hid_codes[:].bitcast(FP4X4),
+                rhs_scale=hid_plane[:],
+                start=True,
+                stop=True,
+            )
+            return sums
+
+        def step(n):
+            damp = work.tile([P, SLOTS], F32, name="damp")
+            gain = work.tile([P, SLOTS], F32, name="gain")
+            gap = work.tile([P, SLOTS], F32, name="gap")
+            if n == 0:
+                nc.scalar.activation(damp[:], first_old[:], ACT.Sigmoid)
+            else:
+                nc.scalar.activation(damp[:], held[n][:].indirect(place_list[:]), ACT.Sigmoid)
+            sums = project(n)
+            nc.vector.tensor_tensor(gain[:], damp[:], rate_rows[:].rearrange("p n j -> p (n j)"), ALU.mult)
+            if n == 0:
+                nc.vector.tensor_tensor(gap[:], first_old[:], sums[:], ALU.subtract)
+            else:
+                values = work.tile([P, SLOTS], F32, name="values")
+                nc.scalar.copy(values[:], sums[:])
+                nc.vector.tensor_tensor(gap[:], held[n][:].indirect(place_list[:]), values[:], ALU.subtract)
+            nc.vector.tensor_tensor(moved[n][:].indirect(place_list[:]), gap[:], gain[:], ALU.mult)
+
+        def add_by_turning(n, cols, result):
+            turned = psum.tile([P, BANK], F32, name="turned", tag=f"bank{TILES - 1 - cols.start // BANK}", bufs=1)
+            blocks = BANK // P
+            for b in range(blocks):
+                src = slice(cols.start + b * P, cols.start + (b + 1) * P)
+                dst = turned[:, b * P : (b + 1) * P]
+                nc.tensor.matmul(dst, held[n][:, src], ident[:], start=(b == 0), stop=False, is_transpose=True)
+            for b in range(blocks):
+                src = slice(cols.start + b * P, cols.start + (b + 1) * P)
+                dst = turned[:, b * P : (b + 1) * P]
+                nc.tensor.matmul(
+                    dst, moved[n][:, src], ident[:], start=False, stop=(b == blocks - 1), is_transpose=True
+                )
+            turned_sb = work.tile([P, BANK], F32, name="turned_sb")
+            nc.scalar.copy(turned_sb[:], turned[:])
+            back = psum.tile([P, BANK], F32, name="back", tag="back")
+            for b in range(blocks):
+                nc.tensor.transpose(back[:, b * P : (b + 1) * P], turned_sb[:, b * P : (b + 1) * P], ident[:])
+            nc.scalar.copy(result[:], back[:])
+
+        for n in range(TILES):
+            step(n)
+        for n in range(TILES):
+            for c in range(T // BANK):
+                cols = slice(c * BANK, (c + 1) * BANK)
+                result = work.tile([P, BANK], F32, name="result")
+                if n < TILES - 1:
+                    add_by_turning(n, cols, result)
+                else:
+                    nc.vector.tensor_tensor(result[:], held[n][:, cols], moved[n][:, cols], ALU.add)
+                nc.sync.dma_start(out[n * P : (n + 1) * P, cols], result[:])

@@ -1,7 +1,6 @@
 from contextlib import ExitStack
 
 import concourse.mybir as mybir
-from concourse.masks import make_identity
 
 K, U, SLOTS, T, E = 512, 2048, 512, 1024, 512
 FLOPS = 2 * K * E * SLOTS
@@ -40,12 +39,20 @@ def tile_attend_storeblend_kernel(tc, wv, hid_words, hid_scales, store, rate, of
         wv_raw = [keep.tile([P, PACK, HALF], F32, name=f"wv_raw{h}") for h in range(2)]
         rate_cols = keep.tile([P, PACK], F32, name="rate_cols")
         ident = keep.tile([P, P], F32, name="ident")
-        warm = keep.tile([P, 1], F32, name="warm")
 
         nc.gpsimd.memset(scale_rows[:].bitcast(I32), 0)
-        make_identity(nc, ident[:])
+        ones = keep.tile([P, 32], F32, name="ones")
+        column_number = keep.tile([P, 32], F32, name="column_number", align_bytes=64)
+        row_number = keep.tile([P, 32], F32, name="row_number", align_bytes=64)
+        nc.vector.memset(ones[:], 1.0)
+        nc.vector.memset(ident[:], 0.0)
+        nc.vector.tensor_tensor_scan(column_number[:], ones[:], ones[:], 0.0, ALU.mult, ALU.add)
+        nc.vector.transpose(row_number[:], column_number[:])
+        for q in range(4):
+            rows = slice(32 * q, 32 * q + 32)
+            nc.vector.tensor_tensor(ident[rows, rows], column_number[rows, :], row_number[rows, :], ALU.is_equal)
         for n in range(TILES):
-            engine = nc.vector if n < 2 else nc.gpsimd
+            engine = nc.vector if n < 1 else nc.gpsimd
             engine.memset(moved[n][:], 0.0)
 
         wv_rows = wv.rearrange("(p j) e -> p j e", j=PACK)
@@ -54,15 +61,15 @@ def tile_attend_storeblend_kernel(tc, wv, hid_words, hid_scales, store, rate, of
                 scale_rows[32 * q : 32 * q + 4, :].bitcast(I32), hid_scales[0, 4 * q : 4 * q + 4, :].bitcast(I32)
             )
         nc.sync.dma_start(rate_cols[:], rate.rearrange("o (p j) -> (o p) j", j=PACK))
-        nc.scalar.activation(warm[:], rate_cols[:, 0:1], ACT.Sigmoid)
         nc.sync.dma_start(held[0][:], store[0:P, :])
         nc.sync.dma_start(place_list[:], offs)
         nc.sync.dma_start(token_list[:], offs2)
         nc.sync.dma_start(words[:].bitcast(I32), hid_words[0].bitcast(I32))
-        for h in range(2):
-            nc.sync.dma_start(wv_raw[h][:], wv_rows[:, :, h * HALF : (h + 1) * HALF])
-        for n in range(1, TILES):
-            nc.sync.dma_start(held[n][:], store[n * P : (n + 1) * P, :])
+        nc.sync.dma_start(wv_raw[0][:], wv_rows[:, :, 0:HALF])
+        nc.sync.dma_start(held[1][:], store[P : 2 * P, :])
+        nc.sync.dma_start(held[2][:], store[2 * P : 3 * P, :])
+        nc.sync.dma_start(wv_raw[1][:], wv_rows[:, :, HALF:E])
+        nc.sync.dma_start(held[3][:], store[3 * P : 4 * P, :])
 
         first_old = keep.tile([P, SLOTS], F32, name="first_old")
         nc.vector.tensor_copy(first_old[:], held[0][:].indirect(place_list[:]))
@@ -76,7 +83,7 @@ def tile_attend_storeblend_kernel(tc, wv, hid_words, hid_scales, store, rate, of
         for j in range(PACK):
             nc.tensor.transpose(rate_bank[:, j, :], rate_cols[:, j : j + 1].to_broadcast([P, P]), ident[:])
         rate_rows = keep.tile([P, P, PACK], F32, name="rate_rows")
-        nc.scalar.activation(rate_rows[:], rate_bank[:].rearrange("p j n -> p n j"), ACT.Copy, scale=-1.0)
+        nc.scalar.activation(rate_rows[:], rate_bank[:].rearrange("p j n -> p n j"), ACT.Copy)
 
         def project(n):
             h, c0 = divmod(n * P, HALF)
@@ -104,21 +111,25 @@ def tile_attend_storeblend_kernel(tc, wv, hid_words, hid_scales, store, rate, of
 
         def step(n):
             damp = work.tile([P, SLOTS], F32, name="damp")
-            gain = work.tile([P, SLOTS], F32, name="gain")
+            gain = work.tile([P, SLOTS], F32, name="gain", bufs=1)
             gap = work.tile([P, SLOTS], F32, name="gap")
+            delta = work.tile([P, SLOTS], F32, name="delta")
             if n == 0:
-                nc.scalar.activation(damp[:], first_old[:], ACT.Sigmoid)
+                old = first_old
             else:
-                nc.scalar.activation(damp[:], held[n][:].indirect(place_list[:]), ACT.Sigmoid)
+                old = work.tile([P, SLOTS], F32, name="old")
+                nc.vector.tensor_copy(old[:], held[n][:].indirect(place_list[:]))
+            nc.scalar.activation(damp[:], old[:], ACT.Sigmoid)
             sums = project(n)
-            nc.vector.tensor_tensor(gain[:], damp[:], rate_rows[:].rearrange("p n j -> p (n j)"), ALU.mult)
-            if n == 0:
-                nc.vector.tensor_tensor(gap[:], first_old[:], sums[:], ALU.subtract)
+            nc.gpsimd.tensor_tensor(gain[:], damp[:], rate_rows[:].rearrange("p n j -> p (n j)"), ALU.mult)
+            if n < 2:
+                nc.vector.tensor_tensor(gap[:], sums[:], old[:], ALU.subtract)
             else:
                 values = work.tile([P, SLOTS], F32, name="values")
                 nc.scalar.copy(values[:], sums[:])
-                nc.vector.tensor_tensor(gap[:], held[n][:].indirect(place_list[:]), values[:], ALU.subtract)
-            nc.vector.tensor_tensor(moved[n][:].indirect(place_list[:]), gap[:], gain[:], ALU.mult)
+                nc.gpsimd.tensor_tensor(gap[:], values[:], old[:], ALU.subtract)
+            nc.gpsimd.tensor_tensor(delta[:], gap[:], gain[:], ALU.mult)
+            nc.vector.tensor_copy(moved[n][:].indirect(place_list[:]), delta[:])
 
         def add_by_turning(n, cols, result):
             turned = psum.tile([P, BANK], F32, name="turned", tag=f"bank{TILES - 1 - cols.start // BANK}", bufs=1)
@@ -146,8 +157,10 @@ def tile_attend_storeblend_kernel(tc, wv, hid_words, hid_scales, store, rate, of
             for c in range(T // BANK):
                 cols = slice(c * BANK, (c + 1) * BANK)
                 result = work.tile([P, BANK], F32, name="result")
-                if n < TILES - 1:
+                if n < 2:
                     add_by_turning(n, cols, result)
+                elif n == 2:
+                    nc.gpsimd.tensor_tensor(result[:], held[n][:, cols], moved[n][:, cols], ALU.add)
                 else:
                     nc.vector.tensor_tensor(result[:], held[n][:, cols], moved[n][:, cols], ALU.add)
                 nc.sync.dma_start(out[n * P : (n + 1) * P, cols], result[:])

@@ -60,16 +60,16 @@ def tile_attend_storeblend_kernel(tc, wv, hid_words, hid_scales, store, rate, of
             nc.scalar.dma_start(
                 scale_rows[32 * q : 32 * q + 4, :].bitcast(I32), hid_scales[0, 4 * q : 4 * q + 4, :].bitcast(I32)
             )
-        nc.sync.dma_start(rate_cols[:], rate.rearrange("o (p j) -> (o p) j", j=PACK))
-        nc.sync.dma_start(held[0][:], store[0:P, :])
         nc.sync.dma_start(place_list[:], offs)
+        nc.sync.dma_start(held[0][:], store[0:P, :])
         nc.sync.dma_start(token_list[:], offs2)
         nc.sync.dma_start(words[:].bitcast(I32), hid_words[0].bitcast(I32))
         nc.sync.dma_start(wv_raw[0][:], wv_rows[:, :, 0:HALF])
-        nc.sync.dma_start(held[1][:], store[P : 2 * P, :])
+        nc.sync.dma_start(rate_cols[:], rate.rearrange("o (p j) -> (o p) j", j=PACK))
         nc.sync.dma_start(held[2][:], store[2 * P : 3 * P, :])
         nc.sync.dma_start(wv_raw[1][:], wv_rows[:, :, HALF:E])
-        nc.sync.dma_start(held[3][:], store[3 * P : 4 * P, :])
+        for n in (1, 3):
+            nc.sync.dma_start(held[n][:], store[n * P : (n + 1) * P, :])
 
         first_old = keep.tile([P, SLOTS], F32, name="first_old")
         nc.vector.tensor_copy(first_old[:], held[0][:].indirect(place_list[:]))
@@ -79,11 +79,18 @@ def tile_attend_storeblend_kernel(tc, wv, hid_words, hid_scales, store, rate, of
         nc.vector.tensor_copy(hid_plane[:], scale_rows[:].indirect(token_list[:]))
         nc.vector.tensor_copy(hid_codes[:], words[:].indirect(token_list[:]))
 
-        rate_bank = psum.tile([P, PACK, P], F32, name="rate_bank", tag="back")
+        rate_bank = psum.tile([P, PACK, P], F32, name="rate_bank", tag="upright")
         for j in range(PACK):
             nc.tensor.transpose(rate_bank[:, j, :], rate_cols[:, j : j + 1].to_broadcast([P, P]), ident[:])
         rate_rows = keep.tile([P, P, PACK], F32, name="rate_rows")
-        nc.scalar.activation(rate_rows[:], rate_bank[:].rearrange("p j n -> p n j"), ACT.Copy)
+        nc.scalar.activation(rate_rows[:], rate_bank[:].rearrange("p j n -> p n j"), ACT.Copy, scale=-1.0)
+
+        minus_rows = rate_rows[:].rearrange("p n j -> p (n j)")
+        column_bank = psum.tile([P, SLOTS // P, P], F32, name="column_bank", tag="upright")
+        for b in range(SLOTS // P):
+            nc.tensor.transpose(column_bank[:, b, :], minus_rows[:, b * P : (b + 1) * P], ident[:])
+        minus_cols = keep.tile([P, SLOTS // P], F32, name="minus_cols")
+        nc.scalar.copy(minus_cols[:], column_bank[:, :, 0])
 
         def project(n):
             h, c0 = divmod(n * P, HALF)
@@ -97,7 +104,7 @@ def tile_attend_storeblend_kernel(tc, wv, hid_words, hid_scales, store, rate, of
             nc.vector.quantize_mx(
                 out=wv_codes[:].bitcast(FP8X4), scales=wv_plane[:], in_=grouped[:].rearrange("p c j -> p (c j)")
             )
-            sums = psum.tile([P, SLOTS], F32, name="sums", tag=f"bank{n}", bufs=1)
+            sums = psum.tile([P, SLOTS], F32, name="sums", tag=f"sums{n % 2}", bufs=1)
             nc.tensor.matmul_mx(
                 out=sums[:],
                 lhsT=wv_codes[:].bitcast(FP8X4),
@@ -109,58 +116,79 @@ def tile_attend_storeblend_kernel(tc, wv, hid_words, hid_scales, store, rate, of
             )
             return sums
 
-        def step(n):
-            damp = work.tile([P, SLOTS], F32, name="damp")
-            gain = work.tile([P, SLOTS], F32, name="gain", bufs=1)
-            gap = work.tile([P, SLOTS], F32, name="gap")
-            delta = work.tile([P, SLOTS], F32, name="delta")
-            if n == 0:
-                old = first_old
-            else:
-                old = work.tile([P, SLOTS], F32, name="old")
-                nc.vector.tensor_copy(old[:], held[n][:].indirect(place_list[:]))
-            nc.scalar.activation(damp[:], old[:], ACT.Sigmoid)
-            sums = project(n)
-            nc.gpsimd.tensor_tensor(gain[:], damp[:], rate_rows[:].rearrange("p n j -> p (n j)"), ALU.mult)
-            if n < 2:
-                nc.vector.tensor_tensor(gap[:], sums[:], old[:], ALU.subtract)
-            else:
-                values = work.tile([P, SLOTS], F32, name="values")
-                nc.scalar.copy(values[:], sums[:])
-                nc.gpsimd.tensor_tensor(gap[:], values[:], old[:], ALU.subtract)
-            nc.gpsimd.tensor_tensor(delta[:], gap[:], gain[:], ALU.mult)
-            nc.vector.tensor_copy(moved[n][:].indirect(place_list[:]), delta[:])
+        def block(b):
+            return slice(b * P, (b + 1) * P)
 
-        def add_by_turning(n, cols, result):
-            turned = psum.tile([P, BANK], F32, name="turned", tag=f"bank{TILES - 1 - cols.start // BANK}", bufs=1)
+        def turn_and_add(bank, first, second):
             blocks = BANK // P
             for b in range(blocks):
-                src = slice(cols.start + b * P, cols.start + (b + 1) * P)
-                dst = turned[:, b * P : (b + 1) * P]
-                nc.tensor.matmul(dst, held[n][:, src], ident[:], start=(b == 0), stop=False, is_transpose=True)
+                nc.tensor.matmul(bank[:, block(b)], first[:, block(b)], ident[:], start=(b == 0), stop=False, is_transpose=True)
             for b in range(blocks):
-                src = slice(cols.start + b * P, cols.start + (b + 1) * P)
-                dst = turned[:, b * P : (b + 1) * P]
                 nc.tensor.matmul(
-                    dst, moved[n][:, src], ident[:], start=False, stop=(b == blocks - 1), is_transpose=True
+                    bank[:, block(b)], second[:, block(b)], ident[:], start=False, stop=(b == blocks - 1), is_transpose=True
                 )
-            turned_sb = work.tile([P, BANK], F32, name="turned_sb")
-            nc.scalar.copy(turned_sb[:], turned[:])
-            back = psum.tile([P, BANK], F32, name="back", tag="back")
-            for b in range(blocks):
-                nc.tensor.transpose(back[:, b * P : (b + 1) * P], turned_sb[:, b * P : (b + 1) * P], ident[:])
-            nc.scalar.copy(result[:], back[:])
 
-        for n in range(TILES):
-            step(n)
-        for n in range(TILES):
+        def scatter(n, gap, factor):
+            nc.vector.tensor_tensor(moved[n][:].indirect(place_list[:]), gap[:], factor[:], ALU.mult)
+
+        def factors_on_vector(n, sums):
+            damp = work.tile([P, SLOTS], F32, name="damp")
+            gain = work.tile([P, SLOTS], F32, name="gain")
+            gap = work.tile([P, SLOTS], F32, name="gap")
+            if n == 0:
+                nc.scalar.activation(damp[:], first_old[:], ACT.Sigmoid)
+                nc.vector.tensor_tensor(gain[:], damp[:], minus_rows, ALU.mult)
+                nc.vector.tensor_tensor(gap[:], first_old[:], sums[:], ALU.subtract)
+            else:
+                nc.scalar.activation(damp[:], held[n][:].indirect(place_list[:]), ACT.Sigmoid)
+                values = work.tile([P, SLOTS], F32, name="values")
+                nc.scalar.copy(values[:], sums[:])
+                nc.vector.tensor_tensor(gap[:], held[n][:].indirect(place_list[:]), values[:], ALU.subtract)
+                nc.vector.tensor_tensor(gain[:], damp[:], minus_rows, ALU.mult)
+            return gap, gain
+
+        def factors_by_turning(n, sums):
+            minus_values = work.tile([P, SLOTS], F32, name="minus_values")
+            nc.scalar.activation(minus_values[:], sums[:], ACT.Copy, scale=-1.0)
+            old = work.tile([P, SLOTS], F32, name="old")
+            nc.vector.tensor_copy(old[:], held[n][:].indirect(place_list[:]))
+            mixed = psum.tile([P, SLOTS], F32, name="mixed", tag="mixed")
+            turn_and_add(mixed, old, minus_values)
+            rated = work.tile([P, SLOTS], F32, name="rated")
+            for b in range(SLOTS // P):
+                nc.scalar.activation(rated[:, block(b)], mixed[:, block(b)], ACT.Copy, scale=minus_cols[:, b : b + 1])
+            gap = work.tile([P, SLOTS], F32, name="gap")
+            for c in range(2):
+                back = psum.tile([P, 2 * P], F32, name="back", tag=f"pair{c}", bufs=1)
+                for b in range(2):
+                    nc.tensor.transpose(back[:, block(b)], rated[:, block(2 * c + b)], ident[:])
+                nc.scalar.copy(gap[:, 2 * c * P : 2 * (c + 1) * P], back[:])
+            damp = work.tile([P, SLOTS], F32, name="damp")
+            nc.scalar.activation(damp[:], old[:], ACT.Sigmoid)
+            return gap, damp
+
+        def finish(n):
             for c in range(T // BANK):
                 cols = slice(c * BANK, (c + 1) * BANK)
                 result = work.tile([P, BANK], F32, name="result")
-                if n < 2:
-                    add_by_turning(n, cols, result)
-                elif n == 2:
-                    nc.gpsimd.tensor_tensor(result[:], held[n][:, cols], moved[n][:, cols], ALU.add)
+                if n < TILES - 1:
+                    tag = f"sums{1 - c}" if n == 0 else f"pair{c}"
+                    turned = psum.tile([P, BANK], F32, name="turned", tag=tag, bufs=1)
+                    turn_and_add(turned, held[n][:, cols], moved[n][:, cols])
+                    turned_sb = work.tile([P, BANK], F32, name="turned_sb")
+                    nc.scalar.copy(turned_sb[:], turned[:])
+                    upright = psum.tile([P, BANK], F32, name="upright", tag="upright")
+                    for b in range(BANK // P):
+                        nc.tensor.transpose(upright[:, block(b)], turned_sb[:, block(b)], ident[:])
+                    nc.scalar.copy(result[:], upright[:])
                 else:
                     nc.vector.tensor_tensor(result[:], held[n][:, cols], moved[n][:, cols], ALU.add)
                 nc.sync.dma_start(out[n * P : (n + 1) * P, cols], result[:])
+
+        scatter(0, *factors_on_vector(0, project(0)))
+        second = factors_on_vector(1, project(1))
+        later = [factors_by_turning(n, project(n)) for n in range(2, TILES)]
+        finish(0)
+        for n, factors in enumerate([second] + later, 1):
+            scatter(n, *factors)
+            finish(n)

@@ -35,10 +35,11 @@ def tile_attend_storeblend_kernel(tc, wv, hid_words, hid_scales, store, rate, of
         words = keep.tile([P, U], U16, name="words", align_bytes=64)
         scale_rows = keep.tile([P, U], U8, name="scale_rows", align_bytes=64)
         held = [keep.tile([P, T], F32, name=f"held{n}") for n in range(TILES)]
-        moved = [keep.tile([P, T], F32, name=f"moved{n}") for n in range(TILES)]
+        moved = [keep.tile([P, T], F32, name=f"moved{n}") for n in range(2)]
         wv_raw = [keep.tile([P, PACK, HALF], F32, name=f"wv_raw{h}") for h in range(2)]
         rate_cols = keep.tile([P, PACK], F32, name="rate_cols")
         ident = keep.tile([P, P], F32, name="ident")
+        warm = keep.tile([P, 1], F32, name="warm")
 
         nc.gpsimd.memset(scale_rows[:].bitcast(I32), 0)
         ones = keep.tile([P, 32], F32, name="ones")
@@ -51,46 +52,38 @@ def tile_attend_storeblend_kernel(tc, wv, hid_words, hid_scales, store, rate, of
         for q in range(4):
             rows = slice(32 * q, 32 * q + 32)
             nc.vector.tensor_tensor(ident[rows, rows], column_number[rows, :], row_number[rows, :], ALU.is_equal)
-        for n in range(TILES):
-            engine = nc.vector if n < 1 else nc.gpsimd
-            engine.memset(moved[n][:], 0.0)
+        for n in range(2):
+            nc.vector.memset(moved[n][:], 0.0)
 
         wv_rows = wv.rearrange("(p j) e -> p j e", j=PACK)
         for q in range(4):
             nc.scalar.dma_start(
                 scale_rows[32 * q : 32 * q + 4, :].bitcast(I32), hid_scales[0, 4 * q : 4 * q + 4, :].bitcast(I32)
             )
-        nc.sync.dma_start(place_list[:], offs)
+        nc.sync.dma_start(rate_cols[:], rate.rearrange("o (p j) -> (o p) j", j=PACK))
+        nc.scalar.activation(warm[:], rate_cols[:, 0:1], ACT.Sigmoid)
         nc.sync.dma_start(held[0][:], store[0:P, :])
+        nc.sync.dma_start(place_list[:], offs)
         nc.sync.dma_start(token_list[:], offs2)
         nc.sync.dma_start(words[:].bitcast(I32), hid_words[0].bitcast(I32))
-        nc.sync.dma_start(wv_raw[0][:], wv_rows[:, :, 0:HALF])
-        nc.sync.dma_start(rate_cols[:], rate.rearrange("o (p j) -> (o p) j", j=PACK))
-        nc.sync.dma_start(held[2][:], store[2 * P : 3 * P, :])
-        nc.sync.dma_start(wv_raw[1][:], wv_rows[:, :, HALF:E])
-        for n in (1, 3):
+        for h in range(2):
+            nc.sync.dma_start(wv_raw[h][:], wv_rows[:, :, h * HALF : (h + 1) * HALF])
+        for n in range(1, TILES):
             nc.sync.dma_start(held[n][:], store[n * P : (n + 1) * P, :])
 
         first_old = keep.tile([P, SLOTS], F32, name="first_old")
         nc.vector.tensor_copy(first_old[:], held[0][:].indirect(place_list[:]))
 
-        hid_codes = keep.tile([P, SLOTS], U16, name="hid_codes", align_bytes=64)
-        hid_plane = keep.tile([P, SLOTS], U8, name="hid_plane", align_bytes=64)
+        hid_codes = keep.tile([P, SLOTS], U16, name="hid_codes", tag="codes_then_moved", align_bytes=64)
+        hid_plane = keep.tile([P, SLOTS], U8, name="hid_plane", tag="plane_then_moved", align_bytes=64)
         nc.vector.tensor_copy(hid_plane[:], scale_rows[:].indirect(token_list[:]))
         nc.vector.tensor_copy(hid_codes[:], words[:].indirect(token_list[:]))
 
-        rate_bank = psum.tile([P, PACK, P], F32, name="rate_bank", tag="upright")
+        rate_bank = psum.tile([P, PACK, P], F32, name="rate_bank", tag="back")
         for j in range(PACK):
             nc.tensor.transpose(rate_bank[:, j, :], rate_cols[:, j : j + 1].to_broadcast([P, P]), ident[:])
         rate_rows = keep.tile([P, P, PACK], F32, name="rate_rows")
         nc.scalar.activation(rate_rows[:], rate_bank[:].rearrange("p j n -> p n j"), ACT.Copy, scale=-1.0)
-
-        minus_rows = rate_rows[:].rearrange("p n j -> p (n j)")
-        column_bank = psum.tile([P, SLOTS // P, P], F32, name="column_bank", tag="upright")
-        for b in range(SLOTS // P):
-            nc.tensor.transpose(column_bank[:, b, :], minus_rows[:, b * P : (b + 1) * P], ident[:])
-        minus_cols = keep.tile([P, SLOTS // P], F32, name="minus_cols")
-        nc.scalar.copy(minus_cols[:], column_bank[:, :, 0])
 
         def project(n):
             h, c0 = divmod(n * P, HALF)
@@ -116,79 +109,60 @@ def tile_attend_storeblend_kernel(tc, wv, hid_words, hid_scales, store, rate, of
             )
             return sums
 
-        def block(b):
-            return slice(b * P, (b + 1) * P)
-
-        def turn_and_add(bank, first, second):
-            blocks = BANK // P
-            for b in range(blocks):
-                nc.tensor.matmul(bank[:, block(b)], first[:, block(b)], ident[:], start=(b == 0), stop=False, is_transpose=True)
-            for b in range(blocks):
-                nc.tensor.matmul(
-                    bank[:, block(b)], second[:, block(b)], ident[:], start=False, stop=(b == blocks - 1), is_transpose=True
-                )
-
-        def scatter(n, gap, factor):
-            nc.vector.tensor_tensor(moved[n][:].indirect(place_list[:]), gap[:], factor[:], ALU.mult)
-
-        def factors_on_vector(n, sums):
+        def step(n):
             damp = work.tile([P, SLOTS], F32, name="damp")
             gain = work.tile([P, SLOTS], F32, name="gain")
             gap = work.tile([P, SLOTS], F32, name="gap")
             if n == 0:
                 nc.scalar.activation(damp[:], first_old[:], ACT.Sigmoid)
-                nc.vector.tensor_tensor(gain[:], damp[:], minus_rows, ALU.mult)
-                nc.vector.tensor_tensor(gap[:], first_old[:], sums[:], ALU.subtract)
             else:
                 nc.scalar.activation(damp[:], held[n][:].indirect(place_list[:]), ACT.Sigmoid)
+            sums = project(n)
+            nc.vector.tensor_tensor(gain[:], damp[:], rate_rows[:].rearrange("p n j -> p (n j)"), ALU.mult)
+            if n == 0:
+                nc.vector.tensor_tensor(gap[:], first_old[:], sums[:], ALU.subtract)
+            else:
                 values = work.tile([P, SLOTS], F32, name="values")
                 nc.scalar.copy(values[:], sums[:])
                 nc.vector.tensor_tensor(gap[:], held[n][:].indirect(place_list[:]), values[:], ALU.subtract)
-                nc.vector.tensor_tensor(gain[:], damp[:], minus_rows, ALU.mult)
             return gap, gain
 
-        def factors_by_turning(n, sums):
-            minus_values = work.tile([P, SLOTS], F32, name="minus_values")
-            nc.scalar.activation(minus_values[:], sums[:], ACT.Copy, scale=-1.0)
-            old = work.tile([P, SLOTS], F32, name="old")
-            nc.vector.tensor_copy(old[:], held[n][:].indirect(place_list[:]))
-            mixed = psum.tile([P, SLOTS], F32, name="mixed", tag="mixed")
-            turn_and_add(mixed, old, minus_values)
-            rated = work.tile([P, SLOTS], F32, name="rated")
-            for b in range(SLOTS // P):
-                nc.scalar.activation(rated[:, block(b)], mixed[:, block(b)], ACT.Copy, scale=minus_cols[:, b : b + 1])
-            gap = work.tile([P, SLOTS], F32, name="gap")
-            for c in range(2):
-                back = psum.tile([P, 2 * P], F32, name="back", tag=f"pair{c}", bufs=1)
-                for b in range(2):
-                    nc.tensor.transpose(back[:, block(b)], rated[:, block(2 * c + b)], ident[:])
-                nc.scalar.copy(gap[:, 2 * c * P : 2 * (c + 1) * P], back[:])
-            damp = work.tile([P, SLOTS], F32, name="damp")
-            nc.scalar.activation(damp[:], old[:], ACT.Sigmoid)
-            return gap, damp
+        def add_by_turning(n, cols, result):
+            turned = psum.tile([P, BANK], F32, name="turned", tag=(f"turned{n}_{cols.start}" if n < 2 else f"sums{cols.start // BANK}"), bufs=1)
+            blocks = BANK // P
+            for b in range(blocks):
+                src = slice(cols.start + b * P, cols.start + (b + 1) * P)
+                dst = turned[:, b * P : (b + 1) * P]
+                nc.tensor.matmul(dst, held[n][:, src], ident[:], start=(b == 0), stop=False, is_transpose=True)
+            for b in range(blocks):
+                src = slice(cols.start + b * P, cols.start + (b + 1) * P)
+                dst = turned[:, b * P : (b + 1) * P]
+                nc.tensor.matmul(
+                    dst, moved[n][:, src], ident[:], start=False, stop=(b == blocks - 1), is_transpose=True
+                )
+            turned_sb = work.tile([P, BANK], F32, name="turned_sb")
+            nc.scalar.copy(turned_sb[:], turned[:])
+            back = psum.tile([P, BANK], F32, name="back", tag="back")
+            for b in range(blocks):
+                nc.tensor.transpose(back[:, b * P : (b + 1) * P], turned_sb[:, b * P : (b + 1) * P], ident[:])
+            nc.scalar.copy(result[:], back[:])
 
-        def finish(n):
+        def scatter(n, gap, gain):
+            nc.vector.tensor_tensor(moved[n][:].indirect(place_list[:]), gap[:], gain[:], ALU.mult)
+
+        scatter(0, *step(0))
+        scatter(1, *step(1))
+        later = [step(n) for n in (2, 3)]
+        for n, tag in ((2, "plane_then_moved"), (3, "codes_then_moved")):
+            moved.append(keep.tile([P, T], F32, name=f"moved{n}", tag=tag, align_bytes=64))
+            nc.gpsimd.memset(moved[n][:], 0.0)
+            scatter(n, *later[n - 2])
+        for n in range(TILES):
             for c in range(T // BANK):
                 cols = slice(c * BANK, (c + 1) * BANK)
                 result = work.tile([P, BANK], F32, name="result")
                 if n < TILES - 1:
-                    tag = f"sums{1 - c}" if n == 0 else f"pair{c}"
-                    turned = psum.tile([P, BANK], F32, name="turned", tag=tag, bufs=1)
-                    turn_and_add(turned, held[n][:, cols], moved[n][:, cols])
-                    turned_sb = work.tile([P, BANK], F32, name="turned_sb")
-                    nc.scalar.copy(turned_sb[:], turned[:])
-                    upright = psum.tile([P, BANK], F32, name="upright", tag="upright")
-                    for b in range(BANK // P):
-                        nc.tensor.transpose(upright[:, block(b)], turned_sb[:, block(b)], ident[:])
-                    nc.scalar.copy(result[:], upright[:])
+                    add_by_turning(n, cols, result)
                 else:
                     nc.vector.tensor_tensor(result[:], held[n][:, cols], moved[n][:, cols], ALU.add)
                 nc.sync.dma_start(out[n * P : (n + 1) * P, cols], result[:])
-
-        scatter(0, *factors_on_vector(0, project(0)))
-        second = factors_on_vector(1, project(1))
-        later = [factors_by_turning(n, project(n)) for n in range(2, TILES)]
-        finish(0)
-        for n, factors in enumerate([second] + later, 1):
-            scatter(n, *factors)
-            finish(n)

@@ -18,52 +18,60 @@ ACT = mybir.ActivationFunctionType
 
 P = 128
 PACK = 4
+QUAD = 32
+QUADS = P // QUAD
+SCALE_ROWS = 4
+LIST_ROWS = 16
+LINE = 4
 BANK = 512
 TILES = E // P
 HALF = E // 2
+PIECES = T // BANK
+TURNED_PIECES = 5
 
 
 def tile_attend_storeblend_kernel(tc, wv, hid_words, hid_scales, store, rate, offs, offs2, out):
     nc = tc.nc
     with ExitStack() as ctx:
         keep = ctx.enter_context(tc.tile_pool(name="keep", bufs=1))
-        work = ctx.enter_context(tc.tile_pool(name="work", bufs=4))
+        work = ctx.enter_context(tc.tile_pool(name="work", bufs=TILES))
         psum = ctx.enter_context(tc.psum_pool(name="psum", bufs=2))
 
-        place_list = keep.tile([P, SLOTS // 16], U16, name="place_list")
-        token_list = keep.tile([P, SLOTS // 16], U16, name="token_list")
+        place_list = keep.tile([P, SLOTS // LIST_ROWS], U16, name="place_list")
+        token_list = keep.tile([P, SLOTS // LIST_ROWS], U16, name="token_list")
         words = keep.tile([P, U], U16, name="words", align_bytes=64)
         scale_rows = keep.tile([P, U], U8, name="scale_rows", align_bytes=64)
         held = [keep.tile([P, T], F32, name=f"held{n}") for n in range(TILES)]
         moved = [keep.tile([P, T], F32, name=f"moved{n}") for n in range(2)]
         wv_raw = [keep.tile([P, PACK, HALF], F32, name=f"wv_raw{h}") for h in range(2)]
-        rate_cols = keep.tile([P, PACK], F32, name="rate_cols")
+        rate_cols = keep.tile([P, SLOTS // P], F32, name="rate_cols")
         ident = keep.tile([P, P], F32, name="ident")
-        warm = keep.tile([P, 1], F32, name="warm")
+        ones = keep.tile([P, QUAD], F32, name="ones")
+        column_number = keep.tile([P, QUAD], F32, name="column_number", align_bytes=64)
+        row_number = keep.tile([P, QUAD], F32, name="row_number", align_bytes=64)
 
         nc.gpsimd.memset(scale_rows[:].bitcast(I32), 0)
-        ones = keep.tile([P, 32], F32, name="ones")
-        column_number = keep.tile([P, 32], F32, name="column_number", align_bytes=64)
-        row_number = keep.tile([P, 32], F32, name="row_number", align_bytes=64)
-        nc.vector.memset(ones[:], 1.0)
-        nc.vector.memset(ident[:], 0.0)
+
+        nc.gpsimd.memset(ones[:], 1.0)
+        nc.gpsimd.memset(ident[:], 0.0)
         nc.vector.tensor_tensor_scan(column_number[:], ones[:], ones[:], 0.0, ALU.mult, ALU.add)
         nc.vector.transpose(row_number[:], column_number[:])
-        for q in range(4):
-            rows = slice(32 * q, 32 * q + 32)
+        for q in range(QUADS):
+            rows = slice(QUAD * q, QUAD * (q + 1))
             nc.vector.tensor_tensor(ident[rows, rows], column_number[rows, :], row_number[rows, :], ALU.is_equal)
+
         for n in range(2):
-            nc.vector.memset(moved[n][:], 0.0)
+            nc.gpsimd.memset(moved[n][:], 0.0)
 
         wv_rows = wv.rearrange("(p j) e -> p j e", j=PACK)
-        for q in range(4):
+        for q in range(QUADS):
             nc.scalar.dma_start(
-                scale_rows[32 * q : 32 * q + 4, :].bitcast(I32), hid_scales[0, 4 * q : 4 * q + 4, :].bitcast(I32)
+                scale_rows[QUAD * q : QUAD * q + SCALE_ROWS, :].bitcast(I32),
+                hid_scales[0, SCALE_ROWS * q : SCALE_ROWS * (q + 1), :].bitcast(I32),
             )
-        nc.sync.dma_start(rate_cols[:], rate.rearrange("o (p j) -> (o p) j", j=PACK))
-        nc.scalar.activation(warm[:], rate_cols[:, 0:1], ACT.Sigmoid)
-        nc.sync.dma_start(held[0][:], store[0:P, :])
         nc.sync.dma_start(place_list[:], offs)
+        nc.sync.dma_start(held[0][:], store[0:P, :])
+        nc.sync.dma_start(rate_cols[:], rate.rearrange("o (p j) -> (o p) j", p=P))
         nc.sync.dma_start(token_list[:], offs2)
         nc.sync.dma_start(words[:].bitcast(I32), hid_words[0].bitcast(I32))
         for h in range(2):
@@ -75,41 +83,41 @@ def tile_attend_storeblend_kernel(tc, wv, hid_words, hid_scales, store, rate, of
         nc.vector.tensor_copy(first_old[:], held[0][:].indirect(place_list[:]))
 
         hid_codes = keep.tile([P, SLOTS], U16, name="hid_codes", tag="codes_then_moved", align_bytes=64)
-        hid_plane = keep.tile([P, SLOTS], U8, name="hid_plane", tag="plane_then_moved", align_bytes=64)
-        nc.vector.tensor_copy(hid_plane[:], scale_rows[:].indirect(token_list[:]))
+        hid_scale = keep.tile([P, SLOTS], U8, name="hid_scale", tag="scale_then_moved", align_bytes=64)
+        nc.vector.tensor_copy(hid_scale[:], scale_rows[:].indirect(token_list[:]))
         nc.vector.tensor_copy(hid_codes[:], words[:].indirect(token_list[:]))
 
-        rate_bank = psum.tile([P, PACK, P], F32, name="rate_bank", tag="back")
-        for j in range(PACK):
+        rate_bank = psum.tile([P, SLOTS // P, P], F32, name="rate_bank", tag="upright")
+        for j in range(SLOTS // P):
             nc.tensor.transpose(rate_bank[:, j, :], rate_cols[:, j : j + 1].to_broadcast([P, P]), ident[:])
-        rate_rows = keep.tile([P, P, PACK], F32, name="rate_rows")
-        nc.scalar.activation(rate_rows[:], rate_bank[:].rearrange("p j n -> p n j"), ACT.Copy, scale=-1.0)
+        minus_rate = keep.tile([P, P, SLOTS // P], F32, name="minus_rate")
+        nc.scalar.activation(minus_rate[:], rate_bank[:].rearrange("p j m -> p m j"), ACT.Copy, scale=-1.0)
 
         def project(n):
             h, c0 = divmod(n * P, HALF)
             grouped = work.tile([P, P, PACK], BF16, name="grouped", align_bytes=64)
             nc.scalar.copy(
-                grouped[:].rearrange("p (c i) j -> p c j i", i=4),
-                wv_raw[h][:, :, c0 : c0 + P].rearrange("p j (c i) -> p c j i", i=4),
+                grouped[:].rearrange("p (c i) j -> p c j i", i=LINE),
+                wv_raw[h][:, :, c0 : c0 + P].rearrange("p j (c i) -> p c j i", i=LINE),
             )
             wv_codes = work.tile([P, P], U32, name="wv_codes", align_bytes=64)
-            wv_plane = work.tile([P, P], U8, name="wv_plane", align_bytes=64)
+            wv_scale = work.tile([P, P], U8, name="wv_scale", align_bytes=64)
             nc.vector.quantize_mx(
-                out=wv_codes[:].bitcast(FP8X4), scales=wv_plane[:], in_=grouped[:].rearrange("p c j -> p (c j)")
+                out=wv_codes[:].bitcast(FP8X4), scales=wv_scale[:], in_=grouped[:].rearrange("p c j -> p (c j)")
             )
             sums = psum.tile([P, SLOTS], F32, name="sums", tag=f"sums{n % 2}", bufs=1)
             nc.tensor.matmul_mx(
                 out=sums[:],
                 lhsT=wv_codes[:].bitcast(FP8X4),
-                lhsT_scale=wv_plane[:],
+                lhsT_scale=wv_scale[:],
                 rhs=hid_codes[:].bitcast(FP4X4),
-                rhs_scale=hid_plane[:],
+                rhs_scale=hid_scale[:],
                 start=True,
                 stop=True,
             )
             return sums
 
-        def step(n):
+        def factors(n):
             damp = work.tile([P, SLOTS], F32, name="damp")
             gain = work.tile([P, SLOTS], F32, name="gain")
             gap = work.tile([P, SLOTS], F32, name="gap")
@@ -118,7 +126,7 @@ def tile_attend_storeblend_kernel(tc, wv, hid_words, hid_scales, store, rate, of
             else:
                 nc.scalar.activation(damp[:], held[n][:].indirect(place_list[:]), ACT.Sigmoid)
             sums = project(n)
-            nc.vector.tensor_tensor(gain[:], damp[:], rate_rows[:].rearrange("p n j -> p (n j)"), ALU.mult)
+            nc.vector.tensor_tensor(gain[:], damp[:], minus_rate[:].rearrange("p m j -> p (m j)"), ALU.mult)
             if n == 0:
                 nc.vector.tensor_tensor(gap[:], first_old[:], sums[:], ALU.subtract)
             else:
@@ -127,42 +135,44 @@ def tile_attend_storeblend_kernel(tc, wv, hid_words, hid_scales, store, rate, of
                 nc.vector.tensor_tensor(gap[:], held[n][:].indirect(place_list[:]), values[:], ALU.subtract)
             return gap, gain
 
-        def add_by_turning(n, cols, result):
-            turned = psum.tile([P, BANK], F32, name="turned", tag=(f"turned{n}_{cols.start}" if n < 2 else f"sums{cols.start // BANK}"), bufs=1)
-            blocks = BANK // P
-            for b in range(blocks):
-                src = slice(cols.start + b * P, cols.start + (b + 1) * P)
-                dst = turned[:, b * P : (b + 1) * P]
-                nc.tensor.matmul(dst, held[n][:, src], ident[:], start=(b == 0), stop=False, is_transpose=True)
-            for b in range(blocks):
-                src = slice(cols.start + b * P, cols.start + (b + 1) * P)
-                dst = turned[:, b * P : (b + 1) * P]
-                nc.tensor.matmul(
-                    dst, moved[n][:, src], ident[:], start=False, stop=(b == blocks - 1), is_transpose=True
-                )
-            turned_sb = work.tile([P, BANK], F32, name="turned_sb")
-            nc.scalar.copy(turned_sb[:], turned[:])
-            back = psum.tile([P, BANK], F32, name="back", tag="back")
-            for b in range(blocks):
-                nc.tensor.transpose(back[:, b * P : (b + 1) * P], turned_sb[:, b * P : (b + 1) * P], ident[:])
-            nc.scalar.copy(result[:], back[:])
-
         def scatter(n, gap, gain):
             nc.vector.tensor_tensor(moved[n][:].indirect(place_list[:]), gap[:], gain[:], ALU.mult)
 
-        scatter(0, *step(0))
-        scatter(1, *step(1))
-        later = [step(n) for n in (2, 3)]
-        for n, tag in ((2, "plane_then_moved"), (3, "codes_then_moved")):
+        def add_by_turning(n, piece, result):
+            tag = f"turned{n}_{piece}" if n < 2 else f"sums{n % 2}"
+            turned = psum.tile([P, BANK], F32, name="turned", tag=tag, bufs=1)
+            blocks = BANK // P
+            for term, source in enumerate((held[n], moved[n])):
+                for b in range(blocks):
+                    nc.tensor.matmul(
+                        turned[:, b * P : (b + 1) * P],
+                        source[:, piece * BANK + b * P : piece * BANK + (b + 1) * P],
+                        ident[:],
+                        start=(term == 0 and b == 0),
+                        stop=(term == 1 and b == blocks - 1),
+                        is_transpose=True,
+                    )
+            turned_sb = work.tile([P, BANK], F32, name="turned_sb")
+            nc.scalar.copy(turned_sb[:], turned[:])
+            upright = psum.tile([P, BANK], F32, name="upright", tag="upright")
+            for b in range(blocks):
+                nc.tensor.transpose(upright[:, b * P : (b + 1) * P], turned_sb[:, b * P : (b + 1) * P], ident[:])
+            nc.scalar.copy(result[:], upright[:])
+
+        scatter(0, *factors(0))
+        scatter(1, *factors(1))
+        later = [factors(n) for n in (2, 3)]
+        for n, tag in ((2, "scale_then_moved"), (3, "codes_then_moved")):
             moved.append(keep.tile([P, T], F32, name=f"moved{n}", tag=tag, align_bytes=64))
             nc.gpsimd.memset(moved[n][:], 0.0)
             scatter(n, *later[n - 2])
+
         for n in range(TILES):
-            for c in range(T // BANK):
-                cols = slice(c * BANK, (c + 1) * BANK)
-                result = work.tile([P, BANK], F32, name="result")
-                if n < TILES - 1:
-                    add_by_turning(n, cols, result)
+            for piece in range(PIECES):
+                cols = slice(piece * BANK, (piece + 1) * BANK)
+                result = work.tile([P, BANK], F32, name="result", bufs=TILES * PIECES)
+                if n * PIECES + piece < TURNED_PIECES:
+                    add_by_turning(n, piece, result)
                 else:
                     nc.vector.tensor_tensor(result[:], held[n][:, cols], moved[n][:, cols], ALU.add)
                 nc.sync.dma_start(out[n * P : (n + 1) * P, cols], result[:])

from contextlib import ExitStack

import concourse.mybir as mybir

K, U, SLOTS, T, E = 512, 2048, 512, 1024, 512
FLOPS = 2 * K * E * SLOTS

F32 = mybir.dt.float32
BF16 = mybir.dt.bfloat16
I32 = mybir.dt.int32
U32 = mybir.dt.uint32
U16 = mybir.dt.uint16
U8 = mybir.dt.uint8
FP8X4 = mybir.dt.float8_e4m3fn_x4
FP4X4 = mybir.dt.float4_e2m1fn_x4
ALU = mybir.AluOpType
ACT = mybir.ActivationFunctionType

P = 128
PACK = 4
QUAD = 32
QUADS = P // QUAD
SCALE_ROWS = 4
LIST_ROWS = 16
LINE = 4
BANK = 512
TILES = E // P
HALF = E // 2
PIECES = T // BANK
TURNED_PIECES = 5


def tile_attend_storeblend_kernel(tc, wv, hid_words, hid_scales, store, rate, offs, offs2, out):
    nc = tc.nc
    with ExitStack() as ctx:
        keep = ctx.enter_context(tc.tile_pool(name="keep", bufs=1))
        work = ctx.enter_context(tc.tile_pool(name="work", bufs=TILES))
        psum = ctx.enter_context(tc.psum_pool(name="psum", bufs=2))

        place_list = keep.tile([P, SLOTS // LIST_ROWS], U16, name="place_list")
        token_list = keep.tile([P, SLOTS // LIST_ROWS], U16, name="token_list")
        words = keep.tile([P, U], U16, name="words", align_bytes=64)
        scale_rows = keep.tile([P, U], U8, name="scale_rows", align_bytes=64)
        held = [keep.tile([P, T], F32, name=f"held{n}") for n in range(TILES)]
        moved = [keep.tile([P, T], F32, name=f"moved{n}") for n in range(2)]
        wv_raw = [keep.tile([P, PACK, HALF], F32, name=f"wv_raw{h}") for h in range(2)]
        rate_cols = keep.tile([P, SLOTS // P], F32, name="rate_cols")
        ident = keep.tile([P, P], F32, name="ident")
        ones = keep.tile([P, QUAD], F32, name="ones")
        column_number = keep.tile([P, QUAD], F32, name="column_number", align_bytes=64)
        row_number = keep.tile([P, QUAD], F32, name="row_number", align_bytes=64)

        nc.gpsimd.memset(scale_rows[:].bitcast(I32), 0)

        nc.gpsimd.memset(ones[:], 1.0)
        nc.gpsimd.memset(ident[:], 0.0)
        nc.vector.tensor_tensor_scan(column_number[:], ones[:], ones[:], 0.0, ALU.mult, ALU.add)
        nc.vector.transpose(row_number[:], column_number[:])
        for q in range(QUADS):
            rows = slice(QUAD * q, QUAD * (q + 1))
            nc.vector.tensor_tensor(ident[rows, rows], column_number[rows, :], row_number[rows, :], ALU.is_equal)

        for n in range(2):
            nc.gpsimd.memset(moved[n][:], 0.0)

        wv_rows = wv.rearrange("(p j) e -> p j e", j=PACK)
        for q in range(QUADS):
            nc.scalar.dma_start(
                scale_rows[QUAD * q : QUAD * q + SCALE_ROWS, :].bitcast(I32),
                hid_scales[0, SCALE_ROWS * q : SCALE_ROWS * (q + 1), :].bitcast(I32),
            )
        nc.sync.dma_start(place_list[:], offs)
        nc.sync.dma_start(held[0][:], store[0:P, :])
        nc.sync.dma_start(rate_cols[:], rate.rearrange("o (p j) -> (o p) j", p=P))
        nc.sync.dma_start(token_list[:], offs2)
        nc.sync.dma_start(words[:].bitcast(I32), hid_words[0].bitcast(I32))
        for h in range(2):
            nc.sync.dma_start(wv_raw[h][:], wv_rows[:, :, h * HALF : (h + 1) * HALF])
        for n in range(1, TILES):
            nc.sync.dma_start(held[n][:], store[n * P : (n + 1) * P, :])

        first_old = keep.tile([P, SLOTS], F32, name="first_old")
        nc.vector.tensor_copy(first_old[:], held[0][:].indirect(place_list[:]))

        hid_codes = keep.tile([P, SLOTS], U16, name="hid_codes", tag="codes_then_moved", align_bytes=64)
        hid_scale = keep.tile([P, SLOTS], U8, name="hid_scale", tag="scale_then_moved", align_bytes=64)
        nc.vector.tensor_copy(hid_scale[:], scale_rows[:].indirect(token_list[:]))
        nc.vector.tensor_copy(hid_codes[:], words[:].indirect(token_list[:]))

        rate_bank = psum.tile([P, SLOTS // P, P], F32, name="rate_bank", tag="upright")
        for j in range(SLOTS // P):
            nc.tensor.transpose(rate_bank[:, j, :], rate_cols[:, j : j + 1].to_broadcast([P, P]), ident[:])
        minus_rate = keep.tile([P, P, SLOTS // P], F32, name="minus_rate")
        nc.scalar.activation(minus_rate[:], rate_bank[:].rearrange("p j m -> p m j"), ACT.Copy, scale=-1.0)

        def project(n):
            h, c0 = divmod(n * P, HALF)
            grouped = work.tile([P, P, PACK], BF16, name="grouped", align_bytes=64)
            nc.scalar.copy(
                grouped[:].rearrange("p (c i) j -> p c j i", i=LINE),
                wv_raw[h][:, :, c0 : c0 + P].rearrange("p j (c i) -> p c j i", i=LINE),
            )
            wv_codes = work.tile([P, P], U32, name="wv_codes", align_bytes=64)
            wv_scale = work.tile([P, P], U8, name="wv_scale", align_bytes=64)
            nc.vector.quantize_mx(
                out=wv_codes[:].bitcast(FP8X4), scales=wv_scale[:], in_=grouped[:].rearrange("p c j -> p (c j)")
            )
            sums = psum.tile([P, SLOTS], F32, name="sums", tag=f"sums{n % 2}", bufs=1)
            nc.tensor.matmul_mx(
                out=sums[:],
                lhsT=wv_codes[:].bitcast(FP8X4),
                lhsT_scale=wv_scale[:],
                rhs=hid_codes[:].bitcast(FP4X4),
                rhs_scale=hid_scale[:],
                start=True,
                stop=True,
            )
            return sums

        def factors(n):
            damp = work.tile([P, SLOTS], F32, name="damp")
            gain = work.tile([P, SLOTS], F32, name="gain")
            gap = work.tile([P, SLOTS], F32, name="gap")
            if n == 0:
                nc.scalar.activation(damp[:], first_old[:], ACT.Sigmoid)
            else:
                nc.scalar.activation(damp[:], held[n][:].indirect(place_list[:]), ACT.Sigmoid)
            sums = project(n)
            nc.vector.tensor_tensor(gain[:], damp[:], minus_rate[:].rearrange("p m j -> p (m j)"), ALU.mult)
            if n == 0:
                nc.vector.tensor_tensor(gap[:], first_old[:], sums[:], ALU.subtract)
            else:
                values = work.tile([P, SLOTS], F32, name="values")
                nc.scalar.copy(values[:], sums[:])
                nc.vector.tensor_tensor(gap[:], held[n][:].indirect(place_list[:]), values[:], ALU.subtract)
            return gap, gain

        def scatter(n, gap, gain):
            nc.vector.tensor_tensor(moved[n][:].indirect(place_list[:]), gap[:], gain[:], ALU.mult)

        def add_by_turning(n, piece, result):
            tag = f"turned{n}_{piece}" if n < 2 else f"sums{n % 2}"
            turned = psum.tile([P, BANK], F32, name="turned", tag=tag, bufs=1)
            blocks = BANK // P
            for term, source in enumerate((held[n], moved[n])):
                for b in range(blocks):
                    nc.tensor.matmul(
                        turned[:, b * P : (b + 1) * P],
                        source[:, piece * BANK + b * P : piece * BANK + (b + 1) * P],
                        ident[:],
                        start=(term == 0 and b == 0),
                        stop=(term == 1 and b == blocks - 1),
                        is_transpose=True,
                    )
            turned_sb = work.tile([P, BANK], F32, name="turned_sb")
            nc.scalar.copy(turned_sb[:], turned[:])
            upright = psum.tile([P, BANK], F32, name="upright", tag="upright")
            for b in range(blocks):
                nc.tensor.transpose(upright[:, b * P : (b + 1) * P], turned_sb[:, b * P : (b + 1) * P], ident[:])
            nc.scalar.copy(result[:], upright[:])

        scatter(0, *factors(0))
        scatter(1, *factors(1))
        later = [factors(n) for n in (2, 3)]
        for n, tag in ((2, "scale_then_moved"), (3, "codes_then_moved")):
            moved.append(keep.tile([P, T], F32, name=f"moved{n}", tag=tag, align_bytes=64))
            nc.gpsimd.memset(moved[n][:], 0.0)
            scatter(n, *later[n - 2])

        for n in range(TILES):
            for piece in range(PIECES):
                cols = slice(piece * BANK, (piece + 1) * BANK)
                result = work.tile([P, BANK], F32, name="result", bufs=TILES * PIECES)
                if n * PIECES + piece < TURNED_PIECES:
                    add_by_turning(n, piece, result)
                else:
                    nc.vector.tensor_tensor(result[:], held[n][:, cols], moved[n][:, cols], ALU.add)
                nc.sync.dma_start(out[n * P : (n + 1) * P, cols], result[:])
